import numpy as np, ml_dtypes
CORES = [13,21,141,149]
N = 4
import mx_ref
NC, K, S = 512, 2, 1
CNT = [[128,56,240,88],[88,240,88,96],[56,184,0,272],[240,32,184,56]]
OFF = [[sum(c[:f]) for f in range(N + 1)] for c in CNT]
BF = ml_dtypes.bfloat16
def setup_inputs(rng):
    def f(*shape):
        return mx_ref.flush((rng.standard_normal(shape, dtype=np.float32) * np.exp2(rng.integers(-2, 3, shape[:-1] + (1,)))).astype(BF))
    return {"w": f(N, 128, 512), "x": f(N, 128, 4 * NC)}
def setup_inputs_blocks(rng):
    d = setup_inputs(rng)
    for k in ("w", "x"): d[k] = mx_ref.spread(d[k], rng, 4)
    return d
def setup_inputs_wide(rng):
    d = setup_inputs(rng)
    for k in ("w", "x"): d[k] = mx_ref.flush((d[k].astype(np.float32) * np.exp2(rng.integers(-8, 9, (N, 1, 1))).astype(np.float32)).astype(BF))
    return d
def setup_inputs_zeros(rng):
    d = setup_inputs(rng); v = d["x"].reshape(N, 128, -1, 4).copy()
    v[np.broadcast_to((rng.random((N, 1, v.shape[2], 1)) < 0.33), v.shape)] = 0
    d["x"] = v.reshape(d["x"].shape)
    return d
def reference(w, x):
    y = np.zeros((N, 128, K * NC), np.float32)
    for e in range(N):
        qw = mx_ref.quantize(w[e])
        for k in range(K):
            f = (e - S * k) % N
            t = np.concatenate([x[j][:, 4 * OFF[j][f]:4 * OFF[j][f + 1]] for j in range(N)], axis=1)
            y[e][:, NC * k:NC * k + NC] = mx_ref.matmul(qw, mx_ref.quantize(t))
    return {"y": y}

@@ -1,0 +1,187 @@
+from concourse.bass import DstId, RemoteDMATransfer
+from concourse.mybir import dt, ActivationFunctionType
+
+N = 4
+NC = 512
+WORLD = 256
+SLOT = 328
+MINCOL = 128
+
+SCRATCH = {
+    "xt": ("sbuf", [128, 4 * NC], "bfloat16"),
+    "wt": ("sbuf", [128, 512], "bfloat16"),
+    "q": ("sbuf", [128, NC], "float8_e4m3fn_x4"),
+    "s": ("sbuf", [128, NC], "uint8"),
+    "qw": ("sbuf", [128, 128], "float8_e4m3fn_x4"),
+    "sw": ("sbuf", [128, 128], "uint8"),
+    "landc": ("sbuf", [128, 3 * SLOT], "float8_e4m3fn_x4"),
+    "lands": ("sbuf", [128, 3 * SLOT], "uint8"),
+    "ps": ("psum", [128, 4 * 512], "float32"),
+    "stage": ("sbuf", [128, 2 * NC], "float32"),
+}
+SEMAPHORES = ["ld0", "ld1", "ldw", "qx", "qw", "rin", "sent", "arr1", "arr2", "arr3",
+              "mm0", "mm1", "mm2", "mm3", "cp0", "cp1", "cp2", "cp3", "sta", "stb"]
+
+
+def _bits(mask):
+    return [i for i in range(mask.bit_length()) if (mask >> i) & 1]
+
+
+def _pack(bits):
+    m = 0
+    for b in bits:
+        m |= 1 << b
+    return m
+
+
+def _helpers(topo, cores, j):
+    c = cores[j]
+    ends = [cores[(j + 1) % N], cores[(j + 3) % N]]
+    port = [h for h in range(WORLD)
+            if h != c and topo.host(h) == topo.host(c) and topo.chip(h) == topo.chip(c)
+            and all(topo.may_write(h, d) for d in ends)]
+    same = [h for h in port if topo.die(h) == topo.die(c)]
+    other = [h for h in port if topo.die(h) != topo.die(c)]
+    return {(1, "c"): same[0], (3, "s"): same[1], (3, "c"): other[0], (1, "s"): other[1]}
+
+
+def _cut(pos, j, k):
+    a = pos[j][2]
+    b = NC - a
+    m = max(a, b)
+    return (a, m, 0, 0) if k == 1 else (b, m, NC - m, m - b)
+
+
+def _view(T, kind, lo, hi, own=False):
+    if kind == "c":
+        return (T.q if own else T.landc)[:, lo:hi].bitcast(dt.uint8)
+    return (T.s if own else T.lands)[:, lo:hi]
+
+
+def rank_program(g, core, T, topo):
+    CNT = T.tables["CNT"]
+    cores = list(T.cores)
+    sem = T.sem
+    pos = [[sum(CNT[j][(j + i) % N] for i in range(k)) for k in range(N + 1)] for j in range(N)]
+    rank = T.rank_of(core)
+
+    if rank is None:
+        for j in range(N):
+            hs = _helpers(topo, cores, j)
+            for (k, kind), h in hs.items():
+                if h != core:
+                    continue
+                n, m, _, lo = _cut(pos, j, k)
+                dst = cores[(j + k) % N]
+                fed = len(_bits(topo.mask(cores[j], core))) // 2
+                eng = _bits(topo.mask(core, dst))
+                rid, pid = topo.addr(dst, core)
+                off = SLOT * (3 - k)
+                g.wait_ge(sem.rin, fed)
+                g.remote_dma(_view(T, kind, off, off + n), _view(T, kind, lo, lo + n),
+                             sem["arr%d" % (N - k)], sem.sent, pid, rid, _pack(eng))
+                g.wait_ge(sem.sent, len(eng))
+        return
+
+    j = rank
+    hs = _helpers(topo, cores, j)
+
+    x0 = sum(CNT[j][:j])
+    wrap = NC - x0
+    mid = wrap if min(wrap, NC - wrap) >= MINCOL else NC // 2
+    chunks = [(0, mid), (mid, NC)]
+    loaders = [g.sync, g.scalar]
+    nld = []
+    for i, (lo, hi) in enumerate(chunks):
+        cuts = [lo] + ([wrap] if lo < wrap < hi else []) + [hi]
+        for p0, p1 in zip(cuts, cuts[1:]):
+            c0 = (p0 + x0) % NC
+            loaders[i].dma_start(T.xt[:, 4 * p0:4 * p1], T.x[:, 4 * c0:4 * (c0 + p1 - p0)]).then_inc(sem["ld%d" % i], 16)
+        nld.append(len(cuts) - 1)
+    g.sync.dma_start(T.wt[:], T.w[:]).then_inc(sem.ldw, 16)
+
+    v = g.vector
+    for i, (lo, hi) in enumerate(chunks):
+        v.wait_ge(sem["ld%d" % i], 16 * nld[i])
+        v.quantize_mx(T.q[:, lo:hi], T.s[:, lo:hi], T.xt[:, 4 * lo:4 * hi]).then_inc(sem.qx, 1)
+    v.wait_ge(sem.ldw, 16)
+    v.quantize_mx(T.qw[:], T.sw[:], T.wt[:]).then_inc(sem.qw, 1)
+
+    g.wait_ge(sem.qx, len(chunks))
+    left = 0
+    for kind in ("c", "s"):
+        trs = []
+        for half, k in enumerate((1, 3)):
+            h = hs[(k, kind)]
+            n, m, t0, _ = _cut(pos, j, k)
+            bits = _bits(topo.mask(core, h))
+            w = len(bits) // 2
+            rid, pid = topo.addr(h, core)
+            trs.append(RemoteDMATransfer(dst_ids=[DstId(rid=rid, pnc=pid)], dma_engine_mask=_pack(bits[half * w:(half + 1) * w]),
+                                         remote_sem=sem.rin, src=_view(T, kind, t0, t0 + m, own=True), dst=_view(T, kind, 0, m)))
+            left += w
+        g.remote_dma_fused(trs, local_sem=sem.sent)
+    dst = cores[(j + 2) % N]
+    eng = _bits(topo.mask(core, dst))
+    rid, pid = topo.addr(dst, core)
+    lo, hi = pos[j][1], pos[j][3]
+    for kind in ("c", "s"):
+        g.remote_dma(_view(T, kind, SLOT, SLOT + hi - lo), _view(T, kind, lo, hi, own=True),
+                     sem.arr2, sem.sent, pid, rid, _pack(eng))
+        left += len(eng)
+    g.wait_ge(sem.sent, left)
+
+    e = j
+    prev = (e - 1) % N
+
+    def width(k):
+        return CNT[(e + k) % N][prev] + CNT[(e + k) % N][e]
+
+    order = [0, 2] + sorted((1, 3), key=width)
+    t = g.tensor
+    t.wait_ge(sem.qx, len(chunks))
+    t.wait_ge(sem.qw, 1)
+    base = 0
+    stores = {"sta": 0, "stb": 0}
+    for bank, k in enumerate(order):
+        src = (e + k) % N
+        c1, c0 = CNT[src][prev], CNT[src][e]
+        y1 = NC + sum(CNT[r][prev] for r in range(src))
+        y0 = sum(CNT[r][e] for r in range(src))
+        p = 512 * bank
+        mm, cp = sem["mm%d" % bank], sem["cp%d" % bank]
+        if k == 0:
+            t.matmul_mx(T.ps[:, p:p + NC], T.qw[:], T.sw[:], T.q[:], T.s[:], True, True).then_inc(mm, 1)
+            moves = [(p + NC - c1, base, c1), (p, base + c1, c0)]
+        else:
+            n = c1 + c0
+            if k == 2:
+                due = 2 * len(_bits(topo.mask(cores[src], core)))
+            else:
+                far = _helpers(topo, cores, src)
+                due = sum(len(_bits(topo.mask(far[(N - k, kind)], core))) for kind in ("c", "s"))
+            off = SLOT * (k - 1)
+            t.wait_ge(sem["arr%d" % k], due)
+            t.matmul_mx(T.ps[:, p:p + n], T.qw[:], T.sw[:], T.landc[:, off:off + n], T.lands[:, off:off + n],
+                        True, True).then_inc(mm, 1)
+            moves = [(p, base, n)]
+        moves = [mv for mv in moves if mv[2] > 0]
+        last = bank == len(order) - 1
+        eng_q = g.scalar if last else g.vector
+        out_q = g.scalar if last else g.sync
+        st_name = "stb" if last else "sta"
+        st = sem[st_name]
+        eng_q.wait_ge(mm, 1)
+        for a, b, c in moves:
+            if last:
+                g.scalar.activation(T.stage[:, b:b + c], T.ps[:, a:a + c], ActivationFunctionType.Copy).then_inc(cp, 1)
+            else:
+                g.vector.tensor_copy(T.stage[:, b:b + c], T.ps[:, a:a + c]).then_inc(cp, 1)
+        out_q.wait_ge(cp, len(moves))
+        for yo, so, c in ((y1, base, c1), (y0, base + c1, c0)):
+            if c > 0:
+                out_q.dma_start(T.y[:, yo:yo + c], T.stage[:, so:so + c]).then_inc(st, 16)
+                stores[st_name] += 1
+        base += c1 + c0
+    g.sync.wait_ge(sem.sta, 16 * stores["sta"])
+    g.scalar.wait_ge(sem.stb, 16 * stores["stb"])

@@ -5,7 +5,6 @@ N = 4
 NC = 512
 WORLD = 256
 SLOT = 328
-MINCOL = 128
 
 SCRATCH = {
     "xt": ("sbuf", [128, 4 * NC], "bfloat16"),
@@ -19,7 +18,7 @@ SCRATCH = {
     "ps": ("psum", [128, 4 * 512], "float32"),
     "stage": ("sbuf", [128, 2 * NC], "float32"),
 }
-SEMAPHORES = ["ld0", "ld1", "ldw", "qx", "qw", "rin", "sent", "arr1", "arr2", "arr3",
+SEMAPHORES = ["ld0", "ld1", "ldw", "q0", "q1", "qw", "rin0", "rin1", "sent", "arr1", "arr2", "arr3",
               "mm0", "mm1", "mm2", "mm3", "cp0", "cp1", "cp2", "cp3", "sta", "stb"]
 
 
@@ -42,7 +41,13 @@ def _helpers(topo, cores, j):
             and all(topo.may_write(h, d) for d in ends)]
     same = [h for h in port if topo.die(h) == topo.die(c)]
     other = [h for h in port if topo.die(h) != topo.die(c)]
-    return {(1, "c"): same[0], (3, "s"): same[1], (3, "c"): other[0], (1, "s"): other[1]}
+    return {("c", 0): same[0], ("c", 1): other[0], ("s", 3): same[1], ("s", 1): other[1]}
+
+
+def _runs(pos, j):
+    a = pos[j][2]
+    first = 1 if a <= NC - a else 3
+    return {1: (0, a), 3: (a, NC)}, (first, N - first)
 
 
 def _cut(pos, j, k):
@@ -50,12 +55,6 @@ def _cut(pos, j, k):
     b = NC - a
     m = max(a, b)
     return (a, m, 0, 0) if k == 1 else (b, m, NC - m, m - b)
-
-
-def _view(T, kind, lo, hi, own=False):
-    if kind == "c":
-        return (T.q if own else T.landc)[:, lo:hi].bitcast(dt.uint8)
-    return (T.s if own else T.lands)[:, lo:hi]
 
 
 def rank_program(g, core, T, topo):
@@ -67,68 +66,98 @@ def rank_program(g, core, T, topo):
 
     if rank is None:
         for j in range(N):
-            hs = _helpers(topo, cores, j)
-            for (k, kind), h in hs.items():
+            for (kind, i), h in _helpers(topo, cores, j).items():
                 if h != core:
                     continue
-                n, m, _, lo = _cut(pos, j, k)
-                dst = cores[(j + k) % N]
                 fed = len(_bits(topo.mask(cores[j], core))) // 2
-                eng = _bits(topo.mask(core, dst))
-                rid, pid = topo.addr(dst, core)
-                off = SLOT * (3 - k)
-                g.wait_ge(sem.rin, fed)
-                g.remote_dma(_view(T, kind, off, off + n), _view(T, kind, lo, lo + n),
-                             sem["arr%d" % (N - k)], sem.sent, pid, rid, _pack(eng))
-                g.wait_ge(sem.sent, len(eng))
+                left = 0
+                if kind == "c":
+                    runs, order = _runs(pos, j)
+                    for idx, k in enumerate(order):
+                        half = (runs[k][1] - runs[k][0]) // 2
+                        dst = cores[(j + k) % N]
+                        eng = _bits(topo.mask(core, dst))
+                        rid, pid = topo.addr(dst, core)
+                        off = SLOT * (3 - k) + i * half
+                        g.wait_ge(sem["rin%d" % idx], fed)
+                        g.remote_dma(T.landc[:, off:off + half].bitcast(dt.uint8),
+                                     T.landc[:, SLOT * idx:SLOT * idx + half].bitcast(dt.uint8),
+                                     sem["arr%d" % (N - k)], sem.sent, pid, rid, _pack(eng))
+                        left += len(eng)
+                else:
+                    k = i
+                    n, m, _, lo = _cut(pos, j, k)
+                    dst = cores[(j + k) % N]
+                    eng = _bits(topo.mask(core, dst))
+                    rid, pid = topo.addr(dst, core)
+                    off = SLOT * (3 - k)
+                    g.wait_ge(sem.rin0, fed)
+                    g.remote_dma(T.lands[:, off:off + n], T.lands[:, lo:lo + n],
+                                 sem["arr%d" % (N - k)], sem.sent, pid, rid, _pack(eng))
+                    left += len(eng)
+                g.wait_ge(sem.sent, left)
         return
 
     j = rank
     hs = _helpers(topo, cores, j)
+    runs, order = _runs(pos, j)
 
     x0 = sum(CNT[j][:j])
     wrap = NC - x0
-    mid = wrap if min(wrap, NC - wrap) >= MINCOL else NC // 2
-    chunks = [(0, mid), (mid, NC)]
-    loaders = [g.sync, g.scalar]
     nld = []
-    for i, (lo, hi) in enumerate(chunks):
+    for idx, k in enumerate(order):
+        lo, hi = runs[k]
         cuts = [lo] + ([wrap] if lo < wrap < hi else []) + [hi]
         for p0, p1 in zip(cuts, cuts[1:]):
             c0 = (p0 + x0) % NC
-            loaders[i].dma_start(T.xt[:, 4 * p0:4 * p1], T.x[:, 4 * c0:4 * (c0 + p1 - p0)]).then_inc(sem["ld%d" % i], 16)
+            g.sync.dma_start(T.xt[:, 4 * p0:4 * p1], T.x[:, 4 * c0:4 * (c0 + p1 - p0)]).then_inc(sem["ld%d" % idx], 16)
         nld.append(len(cuts) - 1)
     g.sync.dma_start(T.wt[:], T.w[:]).then_inc(sem.ldw, 16)
 
     v = g.vector
-    for i, (lo, hi) in enumerate(chunks):
-        v.wait_ge(sem["ld%d" % i], 16 * nld[i])
-        v.quantize_mx(T.q[:, lo:hi], T.s[:, lo:hi], T.xt[:, 4 * lo:4 * hi]).then_inc(sem.qx, 1)
+    for idx, k in enumerate(order):
+        lo, hi = runs[k]
+        v.wait_ge(sem["ld%d" % idx], 16 * nld[idx])
+        v.quantize_mx(T.q[:, lo:hi], T.s[:, lo:hi], T.xt[:, 4 * lo:4 * hi]).then_inc(sem["q%d" % idx], 1)
     v.wait_ge(sem.ldw, 16)
     v.quantize_mx(T.qw[:], T.sw[:], T.wt[:]).then_inc(sem.qw, 1)
 
-    g.wait_ge(sem.qx, len(chunks))
     left = 0
-    for kind in ("c", "s"):
+    for idx, k in enumerate(order):
+        lo, hi = runs[k]
+        half = (hi - lo) // 2
+        g.wait_ge(sem["q%d" % idx], 1)
         trs = []
-        for half, k in enumerate((1, 3)):
-            h = hs[(k, kind)]
-            n, m, t0, _ = _cut(pos, j, k)
+        for i in range(2):
+            h = hs[("c", i)]
             bits = _bits(topo.mask(core, h))
             w = len(bits) // 2
             rid, pid = topo.addr(h, core)
-            trs.append(RemoteDMATransfer(dst_ids=[DstId(rid=rid, pnc=pid)], dma_engine_mask=_pack(bits[half * w:(half + 1) * w]),
-                                         remote_sem=sem.rin, src=_view(T, kind, t0, t0 + m, own=True), dst=_view(T, kind, 0, m)))
+            trs.append(RemoteDMATransfer(dst_ids=[DstId(rid=rid, pnc=pid)], dma_engine_mask=_pack(bits[i * w:(i + 1) * w]),
+                                         remote_sem=sem["rin%d" % idx],
+                                         src=T.q[:, lo + i * half:lo + (i + 1) * half].bitcast(dt.uint8),
+                                         dst=T.landc[:, SLOT * idx:SLOT * idx + half].bitcast(dt.uint8)))
             left += w
         g.remote_dma_fused(trs, local_sem=sem.sent)
+    trs = []
+    for i, k in enumerate((1, 3)):
+        h = hs[("s", k)]
+        n, m, t0, _ = _cut(pos, j, k)
+        bits = _bits(topo.mask(core, h))
+        w = len(bits) // 2
+        rid, pid = topo.addr(h, core)
+        trs.append(RemoteDMATransfer(dst_ids=[DstId(rid=rid, pnc=pid)], dma_engine_mask=_pack(bits[i * w:(i + 1) * w]),
+                                     remote_sem=sem.rin0, src=T.s[:, t0:t0 + m], dst=T.lands[:, 0:m]))
+        left += w
+    g.remote_dma_fused(trs, local_sem=sem.sent)
     dst = cores[(j + 2) % N]
     eng = _bits(topo.mask(core, dst))
     rid, pid = topo.addr(dst, core)
     lo, hi = pos[j][1], pos[j][3]
-    for kind in ("c", "s"):
-        g.remote_dma(_view(T, kind, SLOT, SLOT + hi - lo), _view(T, kind, lo, hi, own=True),
-                     sem.arr2, sem.sent, pid, rid, _pack(eng))
-        left += len(eng)
+    g.remote_dma(T.landc[:, SLOT:SLOT + hi - lo].bitcast(dt.uint8), T.q[:, lo:hi].bitcast(dt.uint8),
+                 sem.arr2, sem.sent, pid, rid, _pack(eng))
+    g.remote_dma(T.lands[:, SLOT:SLOT + hi - lo], T.s[:, lo:hi], sem.arr2, sem.sent, pid, rid, _pack(eng))
+    left += 2 * len(eng)
     g.wait_ge(sem.sent, left)
 
     e = j
@@ -137,13 +166,17 @@ def rank_program(g, core, T, topo):
     def width(k):
         return CNT[(e + k) % N][prev] + CNT[(e + k) % N][e]
 
-    order = [0, 2] + sorted((1, 3), key=width)
+    def late(k):
+        return _runs(pos, (e + k) % N)[1][1] == N - k
+
+    order_in = [0, 2] + sorted((1, 3), key=lambda k: (late(k), width(k)))
     t = g.tensor
-    t.wait_ge(sem.qx, len(chunks))
+    t.wait_ge(sem.q0, 1)
+    t.wait_ge(sem.q1, 1)
     t.wait_ge(sem.qw, 1)
     base = 0
     stores = {"sta": 0, "stb": 0}
-    for bank, k in enumerate(order):
+    for bank, k in enumerate(order_in):
         src = (e + k) % N
         c1, c0 = CNT[src][prev], CNT[src][e]
         y1 = NC + sum(CNT[r][prev] for r in range(src))
@@ -159,14 +192,14 @@ def rank_program(g, core, T, topo):
                 due = 2 * len(_bits(topo.mask(cores[src], core)))
             else:
                 far = _helpers(topo, cores, src)
-                due = sum(len(_bits(topo.mask(far[(N - k, kind)], core))) for kind in ("c", "s"))
+                due = sum(len(_bits(topo.mask(far[key], core))) for key in (("c", 0), ("c", 1), ("s", N - k)))
             off = SLOT * (k - 1)
             t.wait_ge(sem["arr%d" % k], due)
             t.matmul_mx(T.ps[:, p:p + n], T.qw[:], T.sw[:], T.landc[:, off:off + n], T.lands[:, off:off + n],
                         True, True).then_inc(mm, 1)
             moves = [(p, base, n)]
         moves = [mv for mv in moves if mv[2] > 0]
-        last = bank == len(order) - 1
+        last = bank == len(order_in) - 1
         eng_q = g.scalar if last else g.vector
         out_q = g.scalar if last else g.sync
         st_name = "stb" if last else "sta"

from concourse.bass import DstId, RemoteDMATransfer
from concourse.mybir import dt, ActivationFunctionType

N = 4
NC = 512
WORLD = 256
SLOT = 328

SCRATCH = {
    "xt": ("sbuf", [128, 4 * NC], "bfloat16"),
    "wt": ("sbuf", [128, 512], "bfloat16"),
    "q": ("sbuf", [128, NC], "float8_e4m3fn_x4"),
    "s": ("sbuf", [128, NC], "uint8"),
    "qw": ("sbuf", [128, 128], "float8_e4m3fn_x4"),
    "sw": ("sbuf", [128, 128], "uint8"),
    "landc": ("sbuf", [128, 3 * SLOT], "float8_e4m3fn_x4"),
    "lands": ("sbuf", [128, 3 * SLOT], "uint8"),
    "ps": ("psum", [128, 4 * 512], "float32"),
    "stage": ("sbuf", [128, 2 * NC], "float32"),
}
SEMAPHORES = ["ld0", "ld1", "ldw", "q0", "q1", "qw", "rin0", "rin1", "sent", "arr1", "arr2", "arr3",
              "mm0", "mm1", "mm2", "mm3", "cp0", "cp1", "cp2", "cp3", "sta", "stb"]


def _bits(mask):
    return [i for i in range(mask.bit_length()) if (mask >> i) & 1]


def _pack(bits):
    m = 0
    for b in bits:
        m |= 1 << b
    return m


def _helpers(topo, cores, j):
    c = cores[j]
    ends = [cores[(j + 1) % N], cores[(j + 3) % N]]
    port = [h for h in range(WORLD)
            if h != c and topo.host(h) == topo.host(c) and topo.chip(h) == topo.chip(c)
            and all(topo.may_write(h, d) for d in ends)]
    same = [h for h in port if topo.die(h) == topo.die(c)]
    other = [h for h in port if topo.die(h) != topo.die(c)]
    return {("c", 0): same[0], ("c", 1): other[0], ("s", 3): same[1], ("s", 1): other[1]}


def _runs(pos, j):
    a = pos[j][2]
    first = 1 if a <= NC - a else 3
    return {1: (0, a), 3: (a, NC)}, (first, N - first)


def _cut(pos, j, k):
    a = pos[j][2]
    b = NC - a
    m = max(a, b)
    return (a, m, 0, 0) if k == 1 else (b, m, NC - m, m - b)


def rank_program(g, core, T, topo):
    CNT = T.tables["CNT"]
    cores = list(T.cores)
    sem = T.sem
    pos = [[sum(CNT[j][(j + i) % N] for i in range(k)) for k in range(N + 1)] for j in range(N)]
    rank = T.rank_of(core)

    if rank is None:
        for j in range(N):
            for (kind, i), h in _helpers(topo, cores, j).items():
                if h != core:
                    continue
                fed = len(_bits(topo.mask(cores[j], core))) // 2
                left = 0
                if kind == "c":
                    runs, order = _runs(pos, j)
                    for idx, k in enumerate(order):
                        half = (runs[k][1] - runs[k][0]) // 2
                        dst = cores[(j + k) % N]
                        eng = _bits(topo.mask(core, dst))
                        rid, pid = topo.addr(dst, core)
                        off = SLOT * (3 - k) + i * half
                        g.wait_ge(sem["rin%d" % idx], fed)
                        g.remote_dma(T.landc[:, off:off + half].bitcast(dt.uint8),
                                     T.landc[:, SLOT * idx:SLOT * idx + half].bitcast(dt.uint8),
                                     sem["arr%d" % (N - k)], sem.sent, pid, rid, _pack(eng))
                        left += len(eng)
                else:
                    k = i
                    n, m, _, lo = _cut(pos, j, k)
                    dst = cores[(j + k) % N]
                    eng = _bits(topo.mask(core, dst))
                    rid, pid = topo.addr(dst, core)
                    off = SLOT * (3 - k)
                    g.wait_ge(sem.rin0, fed)
                    g.remote_dma(T.lands[:, off:off + n], T.lands[:, lo:lo + n],
                                 sem["arr%d" % (N - k)], sem.sent, pid, rid, _pack(eng))
                    left += len(eng)
                g.wait_ge(sem.sent, left)
        return

    j = rank
    hs = _helpers(topo, cores, j)
    runs, order = _runs(pos, j)

    x0 = sum(CNT[j][:j])
    wrap = NC - x0
    nld = []
    for idx, k in enumerate(order):
        lo, hi = runs[k]
        cuts = [lo] + ([wrap] if lo < wrap < hi else []) + [hi]
        for p0, p1 in zip(cuts, cuts[1:]):
            c0 = (p0 + x0) % NC
            g.sync.dma_start(T.xt[:, 4 * p0:4 * p1], T.x[:, 4 * c0:4 * (c0 + p1 - p0)]).then_inc(sem["ld%d" % idx], 16)
        nld.append(len(cuts) - 1)
    g.sync.dma_start(T.wt[:], T.w[:]).then_inc(sem.ldw, 16)

    v = g.vector
    for idx, k in enumerate(order):
        lo, hi = runs[k]
        v.wait_ge(sem["ld%d" % idx], 16 * nld[idx])
        v.quantize_mx(T.q[:, lo:hi], T.s[:, lo:hi], T.xt[:, 4 * lo:4 * hi]).then_inc(sem["q%d" % idx], 1)
    v.wait_ge(sem.ldw, 16)
    v.quantize_mx(T.qw[:], T.sw[:], T.wt[:]).then_inc(sem.qw, 1)

    left = 0
    for idx, k in enumerate(order):
        lo, hi = runs[k]
        half = (hi - lo) // 2
        g.wait_ge(sem["q%d" % idx], 1)
        trs = []
        for i in range(2):
            h = hs[("c", i)]
            bits = _bits(topo.mask(core, h))
            w = len(bits) // 2
            rid, pid = topo.addr(h, core)
            trs.append(RemoteDMATransfer(dst_ids=[DstId(rid=rid, pnc=pid)], dma_engine_mask=_pack(bits[i * w:(i + 1) * w]),
                                         remote_sem=sem["rin%d" % idx],
                                         src=T.q[:, lo + i * half:lo + (i + 1) * half].bitcast(dt.uint8),
                                         dst=T.landc[:, SLOT * idx:SLOT * idx + half].bitcast(dt.uint8)))
            left += w
        g.remote_dma_fused(trs, local_sem=sem.sent)
    trs = []
    for i, k in enumerate((1, 3)):
        h = hs[("s", k)]
        n, m, t0, _ = _cut(pos, j, k)
        bits = _bits(topo.mask(core, h))
        w = len(bits) // 2
        rid, pid = topo.addr(h, core)
        trs.append(RemoteDMATransfer(dst_ids=[DstId(rid=rid, pnc=pid)], dma_engine_mask=_pack(bits[i * w:(i + 1) * w]),
                                     remote_sem=sem.rin0, src=T.s[:, t0:t0 + m], dst=T.lands[:, 0:m]))
        left += w
    g.remote_dma_fused(trs, local_sem=sem.sent)
    dst = cores[(j + 2) % N]
    eng = _bits(topo.mask(core, dst))
    rid, pid = topo.addr(dst, core)
    lo, hi = pos[j][1], pos[j][3]
    g.remote_dma(T.landc[:, SLOT:SLOT + hi - lo].bitcast(dt.uint8), T.q[:, lo:hi].bitcast(dt.uint8),
                 sem.arr2, sem.sent, pid, rid, _pack(eng))
    g.remote_dma(T.lands[:, SLOT:SLOT + hi - lo], T.s[:, lo:hi], sem.arr2, sem.sent, pid, rid, _pack(eng))
    left += 2 * len(eng)
    g.wait_ge(sem.sent, left)

    e = j
    prev = (e - 1) % N

    def width(k):
        return CNT[(e + k) % N][prev] + CNT[(e + k) % N][e]

    def late(k):
        return _runs(pos, (e + k) % N)[1][1] == N - k

    order_in = [0, 2] + sorted((1, 3), key=lambda k: (late(k), width(k)))
    t = g.tensor
    t.wait_ge(sem.q0, 1)
    t.wait_ge(sem.q1, 1)
    t.wait_ge(sem.qw, 1)
    base = 0
    stores = {"sta": 0, "stb": 0}
    for bank, k in enumerate(order_in):
        src = (e + k) % N
        c1, c0 = CNT[src][prev], CNT[src][e]
        y1 = NC + sum(CNT[r][prev] for r in range(src))
        y0 = sum(CNT[r][e] for r in range(src))
        p = 512 * bank
        mm, cp = sem["mm%d" % bank], sem["cp%d" % bank]
        if k == 0:
            t.matmul_mx(T.ps[:, p:p + NC], T.qw[:], T.sw[:], T.q[:], T.s[:], True, True).then_inc(mm, 1)
            moves = [(p + NC - c1, base, c1), (p, base + c1, c0)]
        else:
            n = c1 + c0
            if k == 2:
                due = 2 * len(_bits(topo.mask(cores[src], core)))
            else:
                far = _helpers(topo, cores, src)
                due = sum(len(_bits(topo.mask(far[key], core))) for key in (("c", 0), ("c", 1), ("s", N - k)))
            off = SLOT * (k - 1)
            t.wait_ge(sem["arr%d" % k], due)
            t.matmul_mx(T.ps[:, p:p + n], T.qw[:], T.sw[:], T.landc[:, off:off + n], T.lands[:, off:off + n],
                        True, True).then_inc(mm, 1)
            moves = [(p, base, n)]
        moves = [mv for mv in moves if mv[2] > 0]
        last = bank == len(order_in) - 1
        eng_q = g.scalar if last else g.vector
        out_q = g.scalar if last else g.sync
        st_name = "stb" if last else "sta"
        st = sem[st_name]
        eng_q.wait_ge(mm, 1)
        for a, b, c in moves:
            if last:
                g.scalar.activation(T.stage[:, b:b + c], T.ps[:, a:a + c], ActivationFunctionType.Copy).then_inc(cp, 1)
            else:
                g.vector.tensor_copy(T.stage[:, b:b + c], T.ps[:, a:a + c]).then_inc(cp, 1)
        out_q.wait_ge(cp, len(moves))
        for yo, so, c in ((y1, base, c1), (y0, base + c1, c0)):
            if c > 0:
                out_q.dma_start(T.y[:, yo:yo + c], T.stage[:, so:so + c]).then_inc(st, 16)
                stores[st_name] += 1
        base += c1 + c0
    g.sync.wait_ge(sem.sta, 16 * stores["sta"])
    g.scalar.wait_ge(sem.stb, 16 * stores["stb"])
